import numpy as np
import ml_dtypes


def mxq(x, axis, fmt="e4m3"):
    dtype, down = {"e4m3": (ml_dtypes.float8_e4m3fn, 7), "e5m2": (ml_dtypes.float8_e5m2, 14)}[fmt]
    v = np.moveaxis(np.asarray(x, np.float32).astype(ml_dtypes.bfloat16).astype(np.float64), axis, -1)
    blocks = v.reshape(v.shape[:-1] + (-1, 32))
    amax = np.abs(blocks).max(-1, keepdims=True)
    byte = np.maximum(np.where(amax > 0, np.frexp(amax)[1] - 1 + 127, 0) - down, 1)
    scale = np.exp2(byte - 127.0)
    codes = (blocks / scale).astype(np.float32).astype(dtype).astype(np.float64)
    return np.moveaxis((codes * scale).reshape(v.shape), -1, axis)


WIDE = False


def mx_kscale(k, group=512):
    if not WIDE:
        return np.ones(k)
    levels = np.array([18, -18])
    if group != 512:
        return np.exp2(np.random.permutation(np.resize(levels, k // group))).repeat(group)
    if k % 512:
        return np.exp2(np.random.permutation(np.resize(levels, k // 32))).repeat(32)
    a = np.empty((k // 512, 16))
    for p in range(k // 512):
        a[p, :8] = np.random.permutation(np.resize(levels, 8))
        for g in range(8):
            far = levels[np.abs(levels - a[p, g]) >= 10]
            a[p, g + 8] = far[np.random.randint(len(far))]
    return np.exp2(a.ravel()).repeat(32)


def f64(x):
    return np.asarray(x).astype(np.float64)


G, D, I, F, E = 8, 128, 128, 128, 128


def sgn(shape):
    return np.random.uniform(0.5, 2.0, shape) * np.where(np.random.standard_normal(shape) < 0, -1.0, 1.0)


def setup_inputs():
    n = np.random.standard_normal
    s_d = mx_kscale(D, 0)
    s_i = mx_kscale(I, 0)
    return {
        "kT": (n((G, D, I)) / np.sqrt(D) / s_d[:, None]).astype(np.float32),
        "S": (n((G, D, E)) * s_d[:, None]).astype(np.float32),
        "v": (n((G, I, E))).astype(np.float32),
        "be": (sgn((G, I, 1)) * s_i[:, None]).astype(np.float32),
        "kn": (n((G, I, F)) / np.sqrt(I) / s_i[:, None] * s_d).astype(np.float32),
    }


def reference(kT, S, v, be, kn):
    kTq = mxq(f64(kT), 1, "e4m3")
    Sq = mxq(f64(S), 1, "e4m3")
    z = kTq.transpose(0, 2, 1) @ Sq
    u = (f64(v) - z) * f64(be)
    knq = mxq(f64(kn), 1, "e4m3")
    uq = mxq(u, 1, "e4m3")
    w = knq.transpose(0, 2, 1) @ uq
    o = f64(S) + w
    return o

@@ -1,0 +1,185 @@
+from contextlib import ExitStack
+
+import concourse.mybir as mybir
+
+G, D = 8, 128
+FLOPS = 2 * 2 * G * D * D * D
+
+F32 = mybir.dt.float32
+BF16 = mybir.dt.bfloat16
+U32 = mybir.dt.uint32
+U8 = mybir.dt.uint8
+FP8X4 = mybir.dt.float8_e4m3fn_x4
+ALU = mybir.AluOpType
+ACT = mybir.ActivationFunctionType
+
+P = 128
+R = 32
+PACK = 4
+TILES = 4
+SETS = 2
+PAD = 64
+K0 = PAD
+S0 = PAD + PACK * D
+S_SPLIT = 32
+
+
+def tile_rows_upd_delta_kernel(tc, kT, S, v, be, kn, out):
+    nc = tc.nc
+    with ExitStack() as ctx:
+        sb = ctx.enter_context(tc.tile_pool(name="sb", bufs=1))
+        ps = ctx.enter_context(tc.psum_pool(name="ps", bufs=1))
+        ctx.enter_context(tc.manual_schedule())
+
+        kt_raw = sb.tile([P, 2, PACK, D], F32, name="kt_raw")
+        s_raw = sb.tile([P, 2, PACK, D], F32, name="s_raw")
+        kn_raw = sb.tile([P, SETS, PACK, D], F32, name="kn_raw")
+        v_raw = sb.tile([P, SETS, PACK, D], F32, name="v_raw")
+        s_rows = sb.tile([P, G, D], F32, name="s_rows")
+        be_t = sb.tile([P, SETS, PACK], F32, name="be_t")
+        kt_bf = sb.tile([P, PACK, D, PACK], BF16, name="kt_bf", align_bytes=64)
+        s_bf = sb.tile([P, 2, D, PACK], BF16, name="s_bf", align_bytes=64)
+        kn_bf = sb.tile([P, SETS, D, PACK], BF16, name="kn_bf", align_bytes=64)
+        u_bf = sb.tile([P, SETS, D, PACK], BF16, name="u_bf", align_bytes=64)
+        c1 = sb.tile([P, S0 + 2 * D], U32, name="c1", align_bytes=64)
+        e1 = sb.tile([P, S0 + 2 * D], U8, name="e1", align_bytes=64)
+        kn_c = sb.tile([P, SETS * D], U32, name="kn_c", align_bytes=64)
+        kn_e = sb.tile([P, SETS * D], U8, name="kn_e", align_bytes=64)
+        u_c = sb.tile([P, SETS * D], U32, name="u_c", align_bytes=64)
+        u_e = sb.tile([P, SETS * D], U8, name="u_e", align_bytes=64)
+        vbe = sb.tile([P, SETS, PACK, D], F32, name="vbe")
+        zbe = sb.tile([P, SETS, PACK, D], F32, name="zbe")
+        res = sb.tile([P, G, D], F32, name="res")
+        banks = [[ps.tile([P, 512], F32, name="bank%d%d" % (r, b)) for b in range(2)] for r in range(TILES)]
+
+        def rows(r):
+            return slice(R * r, R * r + R)
+
+        nc.gpsimd.dma_start(out=be_t[:], in_=be.rearrange("(s c) (p j) o -> (c p) s (j o)", s=SETS, j=PACK))
+        for src, dst in ((kT, kt_raw), (S, s_raw)):
+            for r in range(TILES):
+                eng = nc.sync if r < 2 else nc.scalar
+                eng.dma_start(out=dst[rows(r)], in_=src[2 * r : 2 * r + 2].rearrange("h (p j) w -> p h j w", j=PACK))
+        for src, dst in ((kn, kn_raw), (v, v_raw)):
+            for s in range(SETS):
+                nc.sync.dma_start(out=dst[:, s], in_=src[4 * s : 4 * s + 4].rearrange("c (p j) w -> (c p) j w", j=PACK))
+        for s in range(SETS):
+            nc.sync.dma_start(out=s_rows[:, 4 * s : 4 * s + 4, :], in_=S[4 * s : 4 * s + 4].rearrange("g f e -> f g e"))
+
+        nc.vector.memset(kt_bf[:, 0:3, R : 3 * R, :], 0.0)
+        nc.vector.memset(c1[:, 0:PAD], 0)
+        nc.vector.memset(e1[:, 0:PAD], 127)
+        nc.scalar.activation(out=kt_bf[:, 3, R : 3 * R, :], in_=kt_bf[:, 0, R : 3 * R, :], func=ACT.Copy)
+
+        def deal_kt(h):
+            dst = kt_bf[:, :, 3 * R * h : 3 * R * h + R, :].rearrange("p (a b) t d -> p a t d b", b=2)
+            src = kt_raw[:, h].rearrange("p d (t a b) -> p a t d b", a=2, b=2)
+            return dst, src
+
+        def interleave(dst, src):
+            return (dst.rearrange("p (c i) j -> p c j i", i=2), src.rearrange("p j (c i) -> p c j i", i=2))
+
+        def quantize(codes, scales, values):
+            nc.vector.quantize_mx(out=codes.bitcast(FP8X4), scales=scales, in_=values)
+
+        d0, s0 = deal_kt(0)
+        nc.vector.tensor_copy(out=d0, in_=s0)
+        d1, s1 = deal_kt(1)
+        nc.scalar.copy(out=d1, in_=s1)
+        quantize(c1[:, K0:S0], e1[:, K0:S0], kt_bf[:].rearrange("p a w j -> p (a w j)"))
+
+        d0, s0 = interleave(s_bf[:, 0], s_raw[:, 0])
+        nc.vector.tensor_copy(out=d0, in_=s0)
+        d0, s0 = interleave(s_bf[:, 1, 0:S_SPLIT], s_raw[:, 1, :, 0:S_SPLIT])
+        nc.vector.tensor_copy(out=d0, in_=s0)
+        d0, s0 = interleave(s_bf[:, 1, S_SPLIT:D], s_raw[:, 1, :, S_SPLIT:D])
+        nc.scalar.copy(out=d0, in_=s0)
+        quantize(c1[:, S0:], e1[:, S0:], s_bf[:].rearrange("p h w j -> p (h w j)"))
+
+        for j in range(PACK):
+            for h in range(2):
+                for r in range(TILES):
+                    w0 = K0 + D * j + 2 * R * (h - r % 2)
+                    m0 = S0 + D * h
+                    nc.tensor.matmul_mx(
+                        out=banks[r][j // 2][:, D * (j % 2) : D * (j % 2) + D],
+                        lhsT=c1[rows(r), w0 : w0 + D].bitcast(FP8X4),
+                        lhsT_scale=e1[rows(r), w0 : w0 + D],
+                        rhs=c1[rows(r), m0 : m0 + D].bitcast(FP8X4),
+                        rhs_scale=e1[rows(r), m0 : m0 + D],
+                        start=(h == 0),
+                        stop=(h == 1),
+                    )
+
+        d0, s0 = interleave(kn_bf[:, 0], kn_raw[:, 0])
+        nc.vector.tensor_copy(out=d0, in_=s0)
+        d0, s0 = interleave(kn_bf[:, 1], kn_raw[:, 1])
+        nc.scalar.copy(out=d0, in_=s0)
+        quantize(kn_c[:], kn_e[:], kn_bf[:].rearrange("p h w j -> p (h w j)"))
+
+        for s in range(SETS):
+            for j in range(PACK):
+                nc.gpsimd.tensor_scalar(
+                    out=vbe[:, s, j, :], in0=v_raw[:, s, j, :], scalar1=be_t[:, s, j : j + 1], scalar2=0.0,
+                    op0=ALU.mult, op1=ALU.add,
+                )
+
+        def scale_low(s, b):
+            nc.vector.tensor_tensor(
+                out=zbe[0:64, s, 2 * b : 2 * b + 2, :],
+                in0=banks[2 * s][b][0:64, 0 : 2 * D].rearrange("p (j e) -> p j e", j=2),
+                in1=be_t[0:64, s, 2 * b : 2 * b + 2].unsqueeze(2).to_broadcast([64, 2, D]),
+                op=ALU.mult,
+            )
+
+        def scale_high(s, b):
+            for j in range(2 * b, 2 * b + 2):
+                nc.scalar.activation(
+                    out=zbe[64:P, s, j, :],
+                    in_=banks[2 * s + 1][b][64:P, D * (j % 2) : D * (j % 2) + D],
+                    func=ACT.Copy,
+                    scale=be_t[64:P, s, j : j + 1],
+                )
+
+        def make_u(s):
+            dst, a = interleave(u_bf[:, s], vbe[:, s])
+            dst, b = interleave(u_bf[:, s], zbe[:, s])
+            nc.vector.tensor_tensor(out=dst, in0=a, in1=b, op=ALU.subtract)
+
+        def write_back(s):
+            cols = slice(D * s, D * s + D)
+            quantize(u_c[:, cols], u_e[:, cols], u_bf[:, s].rearrange("p w j -> p (w j)"))
+            for c in range(TILES):
+                nc.tensor.matmul_mx(
+                    out=banks[c][s][:, 2 * D : 3 * D],
+                    lhsT=kn_c[rows(c), cols].bitcast(FP8X4),
+                    lhsT_scale=kn_e[rows(c), cols],
+                    rhs=u_c[rows(c), cols].bitcast(FP8X4),
+                    rhs_scale=u_e[rows(c), cols],
+                    start=True,
+                    stop=True,
+                )
+
+        def finish(s, k):
+            g0 = 4 * s + 2 * k
+            for g in range(g0, g0 + 2):
+                nc.vector.tensor_tensor(
+                    out=res[:, g, :], in0=banks[g % 4][s][:, 2 * D : 3 * D], in1=s_rows[:, g, :], op=ALU.add
+                )
+            nc.sync.dma_start(out=out[g0 : g0 + 2].rearrange("g f e -> f g e"), in_=res[:, g0 : g0 + 2, :])
+
+        for s in range(SETS):
+            for b in range(2):
+                scale_high(s, b)
+        scale_low(0, 0)
+        scale_low(1, 0)
+        scale_low(0, 1)
+        make_u(0)
+        scale_low(1, 1)
+        write_back(0)
+        make_u(1)
+        finish(0, 0)
+        write_back(1)
+        finish(0, 1)
+        finish(1, 0)
+        finish(1, 1)

@@ -18,7 +18,9 @@ R = 32
 PACK = 4
 TILES = 4
 SETS = 2
-PAD = 64
+PAD = 128
+WARM_EARLY = 28
+WARM_LATE = 8
 K0 = PAD
 S0 = PAD + PACK * D
 S_SPLIT = 32
@@ -50,43 +52,64 @@ def tile_rows_upd_delta_kernel(tc, kT, S, v, be, kn, out):
         vbe = sb.tile([P, SETS, PACK, D], F32, name="vbe")
         zbe = sb.tile([P, SETS, PACK, D], F32, name="zbe")
         res = sb.tile([P, G, D], F32, name="res")
-        banks = [[ps.tile([P, 512], F32, name="bank%d%d" % (r, b)) for b in range(2)] for r in range(TILES)]
+        zeros = sb.tile([P, PAD * PACK], BF16, name="zeros", align_bytes=64)
+        warm = ps.tile([P, 512], F32, name="warm")
+        bank0 = ps.tile([P, 512], F32, name="bank0")
+        banks = [[ps.tile([P, 512], F32, name="bank%d%d" % (r, b)) for b in range(2)] if r else [bank0, bank0]
+                 for r in range(TILES)]
+
+        def z_out(r, j):
+            c0 = D * j if r == 0 else D * (j % 2)
+            return banks[r][j // 2][:, c0 : c0 + D]
+
+        def w_out(c, s):
+            c0 = D * s if c == 0 else 2 * D
+            return banks[c][s][:, c0 : c0 + D]
 
         def rows(r):
             return slice(R * r, R * r + R)
 
-        nc.gpsimd.dma_start(out=be_t[:], in_=be.rearrange("(s c) (p j) o -> (c p) s (j o)", s=SETS, j=PACK))
-        for src, dst in ((kT, kt_raw), (S, s_raw)):
+        for src, dst in ((S, s_raw), (kT, kt_raw)):
             for r in range(TILES):
                 eng = nc.sync if r < 2 else nc.scalar
                 eng.dma_start(out=dst[rows(r)], in_=src[2 * r : 2 * r + 2].rearrange("h (p j) w -> p h j w", j=PACK))
-        for src, dst in ((kn, kn_raw), (v, v_raw)):
+        nc.sync.dma_start(out=be_t[:], in_=be.rearrange("(s c) (p j) o -> (c p) s (j o)", s=SETS, j=PACK))
+        for src, dst in ((v, v_raw), (kn, kn_raw)):
             for s in range(SETS):
                 nc.sync.dma_start(out=dst[:, s], in_=src[4 * s : 4 * s + 4].rearrange("c (p j) w -> (c p) j w", j=PACK))
         for s in range(SETS):
             nc.sync.dma_start(out=s_rows[:, 4 * s : 4 * s + 4, :], in_=S[4 * s : 4 * s + 4].rearrange("g f e -> f g e"))
 
-        nc.vector.memset(kt_bf[:, 0:3, R : 3 * R, :], 0.0)
-        nc.vector.memset(c1[:, 0:PAD], 0)
-        nc.vector.memset(e1[:, 0:PAD], 127)
-        nc.scalar.activation(out=kt_bf[:, 3, R : 3 * R, :], in_=kt_bf[:, 0, R : 3 * R, :], func=ACT.Copy)
+        def quantize(codes, scales, values):
+            nc.vector.quantize_mx(out=codes.bitcast(FP8X4), scales=scales, in_=values)
 
-        def deal_kt(h):
-            dst = kt_bf[:, :, 3 * R * h : 3 * R * h + R, :].rearrange("p (a b) t d -> p a t d b", b=2)
-            src = kt_raw[:, h].rearrange("p d (t a b) -> p a t d b", a=2, b=2)
+        def warm_up(w0, passes):
+            for i in range(passes):
+                nc.tensor.matmul_mx(
+                    out=warm[:, D * (i % 4) : D * (i % 4) + D],
+                    lhsT=c1[:, w0 : w0 + D].bitcast(FP8X4),
+                    lhsT_scale=e1[:, w0 : w0 + D],
+                    rhs=c1[:, w0 : w0 + D].bitcast(FP8X4),
+                    rhs_scale=e1[:, w0 : w0 + D],
+                    start=True,
+                    stop=True,
+                )
+
+        nc.vector.memset(zeros[:].bitcast(U32), 0)
+        nc.vector.memset(kt_bf[:, 0:3, R : 3 * R, :].rearrange("p a w j -> p a (w j)").bitcast(U32), 0)
+        quantize(c1[:, 0:PAD], e1[:, 0:PAD], zeros[:])
+        nc.scalar.activation(
+            out=kt_bf[:, 3, R : 3 * R, :].rearrange("p w j -> p (w j)"), in_=zeros[:, 0 : 2 * R * PACK], func=ACT.Copy
+        )
+        warm_up(0, WARM_EARLY)
+
+        def deal_kt(h, a):
+            dst = kt_bf[:, 2 * a : 2 * a + 2, 3 * R * h : 3 * R * h + R, :].rearrange("p b t d -> p t d b")
+            src = kt_raw[:, h].rearrange("p d (t a b) -> p a t d b", a=2, b=2)[:, a]
             return dst, src
 
         def interleave(dst, src):
             return (dst.rearrange("p (c i) j -> p c j i", i=2), src.rearrange("p j (c i) -> p c j i", i=2))
-
-        def quantize(codes, scales, values):
-            nc.vector.quantize_mx(out=codes.bitcast(FP8X4), scales=scales, in_=values)
-
-        d0, s0 = deal_kt(0)
-        nc.vector.tensor_copy(out=d0, in_=s0)
-        d1, s1 = deal_kt(1)
-        nc.scalar.copy(out=d1, in_=s1)
-        quantize(c1[:, K0:S0], e1[:, K0:S0], kt_bf[:].rearrange("p a w j -> p (a w j)"))
 
         d0, s0 = interleave(s_bf[:, 0], s_raw[:, 0])
         nc.vector.tensor_copy(out=d0, in_=s0)
@@ -95,14 +118,24 @@ def tile_rows_upd_delta_kernel(tc, kT, S, v, be, kn, out):
         d0, s0 = interleave(s_bf[:, 1, S_SPLIT:D], s_raw[:, 1, :, S_SPLIT:D])
         nc.scalar.copy(out=d0, in_=s0)
         quantize(c1[:, S0:], e1[:, S0:], s_bf[:].rearrange("p h w j -> p (h w j)"))
+        warm_up(S0, WARM_LATE)
 
-        for j in range(PACK):
+        for a in range(2):
+            d0, s0 = deal_kt(0, a)
+            nc.vector.tensor_copy(out=d0, in_=s0)
+            d0, s0 = deal_kt(1, a)
+            nc.scalar.copy(out=d0, in_=s0)
+        for a in range(2):
+            words = slice(K0 + 2 * D * a, K0 + 2 * D * (a + 1))
+            quantize(c1[:, words], e1[:, words], kt_bf[:, 2 * a : 2 * a + 2].rearrange("p a w j -> p (a w j)"))
+
+        for s, j in [(s, j) for s in range(SETS) for j in range(PACK)]:
             for h in range(2):
-                for r in range(TILES):
+                for r in (2 * s, 2 * s + 1):
                     w0 = K0 + D * j + 2 * R * (h - r % 2)
                     m0 = S0 + D * h
                     nc.tensor.matmul_mx(
-                        out=banks[r][j // 2][:, D * (j % 2) : D * (j % 2) + D],
+                        out=z_out(r, j),
                         lhsT=c1[rows(r), w0 : w0 + D].bitcast(FP8X4),
                         lhsT_scale=e1[rows(r), w0 : w0 + D],
                         rhs=c1[rows(r), m0 : m0 + D].bitcast(FP8X4),
@@ -111,34 +144,36 @@ def tile_rows_upd_delta_kernel(tc, kT, S, v, be, kn, out):
                         stop=(h == 1),
                     )
 
-        d0, s0 = interleave(kn_bf[:, 0], kn_raw[:, 0])
-        nc.vector.tensor_copy(out=d0, in_=s0)
-        d0, s0 = interleave(kn_bf[:, 1], kn_raw[:, 1])
-        nc.scalar.copy(out=d0, in_=s0)
-        quantize(kn_c[:], kn_e[:], kn_bf[:].rearrange("p h w j -> p (h w j)"))
+        def copy_kn(s):
+            dst, src = interleave(kn_bf[:, s], kn_raw[:, s])
+            nc.vector.tensor_copy(out=dst, in_=src)
 
-        for s in range(SETS):
+        def quantize_kn(s):
+            cols = slice(D * s, D * s + D)
+            quantize(kn_c[:, cols], kn_e[:, cols], kn_bf[:, s].rearrange("p w j -> p (w j)"))
+
+        def scale_v(s):
             for j in range(PACK):
-                nc.gpsimd.tensor_scalar(
-                    out=vbe[:, s, j, :], in0=v_raw[:, s, j, :], scalar1=be_t[:, s, j : j + 1], scalar2=0.0,
-                    op0=ALU.mult, op1=ALU.add,
+                nc.scalar.activation(
+                    out=vbe[:, s, j, :], in_=v_raw[:, s, j, :], func=ACT.Copy, scale=be_t[:, s, j : j + 1]
                 )
 
-        def scale_low(s, b):
+        def scale_low(s, j0, n):
             nc.vector.tensor_tensor(
-                out=zbe[0:64, s, 2 * b : 2 * b + 2, :],
-                in0=banks[2 * s][b][0:64, 0 : 2 * D].rearrange("p (j e) -> p j e", j=2),
-                in1=be_t[0:64, s, 2 * b : 2 * b + 2].unsqueeze(2).to_broadcast([64, 2, D]),
+                out=zbe[0:64, s, j0 : j0 + n, :],
+                in0=banks[2 * s][j0 // 2][0:64, 0 : n * D].rearrange("p (j e) -> p j e", j=n),
+                in1=be_t[0:64, s, j0 : j0 + n].unsqueeze(2).to_broadcast([64, n, D]),
                 op=ALU.mult,
             )
 
-        def scale_high(s, b):
+        def scale_act(r, b):
+            half = slice(64 * (r % 2), 64 * (r % 2) + 64)
             for j in range(2 * b, 2 * b + 2):
                 nc.scalar.activation(
-                    out=zbe[64:P, s, j, :],
-                    in_=banks[2 * s + 1][b][64:P, D * (j % 2) : D * (j % 2) + D],
+                    out=zbe[half, r // 2, j, :],
+                    in_=banks[r][b][half, D * (j % 2) : D * (j % 2) + D],
                     func=ACT.Copy,
-                    scale=be_t[64:P, s, j : j + 1],
+                    scale=be_t[half, r // 2, j : j + 1],
                 )
 
         def make_u(s):
@@ -151,7 +186,7 @@ def tile_rows_upd_delta_kernel(tc, kT, S, v, be, kn, out):
             quantize(u_c[:, cols], u_e[:, cols], u_bf[:, s].rearrange("p w j -> p (w j)"))
             for c in range(TILES):
                 nc.tensor.matmul_mx(
-                    out=banks[c][s][:, 2 * D : 3 * D],
+                    out=w_out(c, s),
                     lhsT=kn_c[rows(c), cols].bitcast(FP8X4),
                     lhsT_scale=kn_e[rows(c), cols],
                     rhs=u_c[rows(c), cols].bitcast(FP8X4),
@@ -164,22 +199,24 @@ def tile_rows_upd_delta_kernel(tc, kT, S, v, be, kn, out):
             g0 = 4 * s + 2 * k
             for g in range(g0, g0 + 2):
                 nc.vector.tensor_tensor(
-                    out=res[:, g, :], in0=banks[g % 4][s][:, 2 * D : 3 * D], in1=s_rows[:, g, :], op=ALU.add
+                    out=res[:, g, :], in0=w_out(g % 4, s), in1=s_rows[:, g, :], op=ALU.add
                 )
             nc.sync.dma_start(out=out[g0 : g0 + 2].rearrange("g f e -> f g e"), in_=res[:, g0 : g0 + 2, :])
 
-        for s in range(SETS):
-            for b in range(2):
-                scale_high(s, b)
-        scale_low(0, 0)
-        scale_low(1, 0)
-        scale_low(0, 1)
+        scale_v(0)
+        scale_v(1)
+        for r, b in ((1, 0), (1, 1), (3, 0), (2, 0), (3, 1)):
+            scale_act(r, b)
+        copy_kn(0)
+        quantize_kn(0)
+        copy_kn(1)
+        scale_low(0, 0, 4)
         make_u(0)
-        scale_low(1, 1)
+        scale_low(1, 2, 2)
         write_back(0)
         make_u(1)
-        finish(0, 0)
+        quantize_kn(1)
         write_back(1)
-        finish(0, 1)
-        finish(1, 0)
-        finish(1, 1)
+        for s in range(SETS):
+            for k in range(2):
+                finish(s, k)

@@ -8,6 +8,7 @@ FLOPS = 2 * 2 * G * D * D * D
 F32 = mybir.dt.float32
 BF16 = mybir.dt.bfloat16
 U32 = mybir.dt.uint32
+I32 = mybir.dt.int32
 U8 = mybir.dt.uint8
 FP8X4 = mybir.dt.float8_e4m3fn_x4
 ALU = mybir.AluOpType
@@ -38,13 +39,14 @@ def tile_rows_upd_delta_kernel(tc, kT, S, v, be, kn, out):
         kn_raw = sb.tile([P, SETS, PACK, D], F32, name="kn_raw")
         v_raw = sb.tile([P, SETS, PACK, D], F32, name="v_raw")
         s_rows = sb.tile([P, G, D], F32, name="s_rows")
-        be_t = sb.tile([P, SETS, PACK], F32, name="be_t")
-        kt_bf = sb.tile([P, PACK, D, PACK], BF16, name="kt_bf", align_bytes=64)
+        be_t = sb.tile([P, SETS, PACK, 1], F32, name="be_t")
+        kt_bf = sb.tile([P, 2, PACK, 2, R, PACK], BF16, name="kt_bf", align_bytes=64)
         s_bf = sb.tile([P, 2, D, PACK], BF16, name="s_bf", align_bytes=64)
         kn_bf = sb.tile([P, SETS, D, PACK], BF16, name="kn_bf", align_bytes=64)
         u_bf = sb.tile([P, SETS, D, PACK], BF16, name="u_bf", align_bytes=64)
         c1 = sb.tile([P, S0 + 2 * D], U32, name="c1", align_bytes=64)
         e1 = sb.tile([P, S0 + 2 * D], U8, name="e1", align_bytes=64)
+        e2 = sb.tile([P, S0 + R], U8, name="e2", align_bytes=64)
         kn_c = sb.tile([P, SETS * D], U32, name="kn_c", align_bytes=64)
         kn_e = sb.tile([P, SETS * D], U8, name="kn_e", align_bytes=64)
         u_c = sb.tile([P, SETS * D], U32, name="u_c", align_bytes=64)
@@ -66,19 +68,37 @@ def tile_rows_upd_delta_kernel(tc, kT, S, v, be, kn, out):
             c0 = D * s if c == 0 else 2 * D
             return banks[c][s][:, c0 : c0 + D]
 
+        def pair(t, r):
+            return t[r : r + 5 : 4].rearrange("g f e -> f g e")
+
+        def quadrant(r, h):
+            return 2 + h if r % 2 else 1 - h
+
         def rows(r):
             return slice(R * r, R * r + R)
 
+        def by_rows(src):
+            return src.rearrange("c (p j) w -> (c p) j w", j=PACK)
+
+        def load_tokens(eng, dst, src, part):
+            lo, hi, g0 = ((0, R, 4), (R, 3 * R, 0), (3 * R, P, 5))[part]
+            heads = src.rearrange("(h s c) (p j) w -> h c p s j w", h=2, s=SETS, j=PACK)
+            if part == 1:
+                view = heads[0].rearrange("c p s j w -> (c p) s j w")
+            else:
+                view = heads[1, g0 - 4]
+            eng.dma_start(out=dst[lo:hi], in_=view)
+
         for src, dst in ((S, s_raw), (kT, kt_raw)):
-            for r in range(TILES):
-                eng = nc.sync if r < 2 else nc.scalar
-                eng.dma_start(out=dst[rows(r)], in_=src[2 * r : 2 * r + 2].rearrange("h (p j) w -> p h j w", j=PACK))
-        nc.sync.dma_start(out=be_t[:], in_=be.rearrange("(s c) (p j) o -> (c p) s (j o)", s=SETS, j=PACK))
+            for h in range(2):
+                nc.sync.dma_start(out=dst[:, h], in_=by_rows(src[4 * h : 4 * h + 4]))
+        for part in range(3):
+            load_tokens(nc.scalar, be_t, be, part)
         for src, dst in ((v, v_raw), (kn, kn_raw)):
-            for s in range(SETS):
-                nc.sync.dma_start(out=dst[:, s], in_=src[4 * s : 4 * s + 4].rearrange("c (p j) w -> (c p) j w", j=PACK))
-        for s in range(SETS):
-            nc.sync.dma_start(out=s_rows[:, 4 * s : 4 * s + 4, :], in_=S[4 * s : 4 * s + 4].rearrange("g f e -> f g e"))
+            for part in (0, 2, 1):
+                load_tokens(nc.sync, dst, src, part)
+        for r in range(TILES):
+            nc.sync.dma_start(out=s_rows[:, 2 * r : 2 * r + 2, :], in_=pair(S, r))
 
         def quantize(codes, scales, values):
             nc.vector.quantize_mx(out=codes.bitcast(FP8X4), scales=scales, in_=values)
@@ -96,48 +116,66 @@ def tile_rows_upd_delta_kernel(tc, kT, S, v, be, kn, out):
                 )
 
         nc.vector.memset(zeros[:].bitcast(U32), 0)
-        nc.vector.memset(kt_bf[:, 0:3, R : 3 * R, :].rearrange("p a w j -> p a (w j)").bitcast(U32), 0)
+        blocks = kt_bf[:].rearrange("p h a z t j -> p (h a) z (t j)")
+        nc.vector.memset(blocks[:, 0:6, 1, :].bitcast(U32), 0)
         quantize(c1[:, 0:PAD], e1[:, 0:PAD], zeros[:])
+        nc.vector.memset(e1[:, K0:S0].bitcast(I32), 0)
+        nc.vector.memset(e2[:].bitcast(I32), 0)
         nc.scalar.activation(
-            out=kt_bf[:, 3, R : 3 * R, :].rearrange("p w j -> p (w j)"), in_=zeros[:, 0 : 2 * R * PACK], func=ACT.Copy
+            out=blocks[:, 6:8, 1, :], in_=zeros[:, 0 : 2 * R * PACK].rearrange("p (a w) -> p a w", a=2), func=ACT.Copy
         )
         warm_up(0, WARM_EARLY)
 
         def deal_kt(h, a):
-            dst = kt_bf[:, 2 * a : 2 * a + 2, 3 * R * h : 3 * R * h + R, :].rearrange("p b t d -> p t d b")
+            dst = kt_bf[:, h, 2 * a : 2 * a + 2, 0].rearrange("p b t d -> p t d b")
             src = kt_raw[:, h].rearrange("p d (t a b) -> p a t d b", a=2, b=2)[:, a]
             return dst, src
 
         def interleave(dst, src):
             return (dst.rearrange("p (c i) j -> p c j i", i=2), src.rearrange("p j (c i) -> p c j i", i=2))
 
-        d0, s0 = interleave(s_bf[:, 0], s_raw[:, 0])
-        nc.vector.tensor_copy(out=d0, in_=s0)
-        d0, s0 = interleave(s_bf[:, 1, 0:S_SPLIT], s_raw[:, 1, :, 0:S_SPLIT])
-        nc.vector.tensor_copy(out=d0, in_=s0)
-        d0, s0 = interleave(s_bf[:, 1, S_SPLIT:D], s_raw[:, 1, :, S_SPLIT:D])
-        nc.scalar.copy(out=d0, in_=s0)
+        for h in range(2):
+            d0, s0 = interleave(s_bf[:, h], s_raw[:, h])
+            nc.vector.tensor_copy(out=d0, in_=s0)
         quantize(c1[:, S0:], e1[:, S0:], s_bf[:].rearrange("p h w j -> p (h w j)"))
         warm_up(S0, WARM_LATE)
 
+        d0, s0 = deal_kt(0, 0)
+        nc.vector.tensor_copy(out=d0, in_=s0)
+        d0, s0 = deal_kt(0, 1)
+        nc.scalar.copy(out=d0, in_=s0)
+
+        def quantize_kt(h, a0, n):
+            words = slice(K0 + 2 * D * h + D * a0, K0 + 2 * D * h + D * (a0 + n))
+            values = kt_bf[:, h, 2 * a0 : 2 * (a0 + n)].rearrange("p a z t j -> p (a z t j)")
+            quantize(c1[:, words], e1[:, words], values)
+
+        def shift_scales(h, a0, n):
+            w0 = K0 + 2 * D * h + D * a0
+            nc.vector.tensor_copy(
+                out=e2[:, w0 + R : w0 + R + D * n].bitcast(I32), in_=e1[:, w0 : w0 + D * n].bitcast(I32)
+            )
+
+        quantize_kt(0, 0, 2)
+        shift_scales(0, 0, 2)
         for a in range(2):
-            d0, s0 = deal_kt(0, a)
-            nc.vector.tensor_copy(out=d0, in_=s0)
             d0, s0 = deal_kt(1, a)
-            nc.scalar.copy(out=d0, in_=s0)
+            nc.vector.tensor_copy(out=d0, in_=s0)
         for a in range(2):
-            words = slice(K0 + 2 * D * a, K0 + 2 * D * (a + 1))
-            quantize(c1[:, words], e1[:, words], kt_bf[:, 2 * a : 2 * a + 2].rearrange("p a w j -> p (a w j)"))
+            quantize_kt(1, a, 1)
+        for a in range(2):
+            shift_scales(1, a, 1)
 
         for s, j in [(s, j) for s in range(SETS) for j in range(PACK)]:
             for h in range(2):
                 for r in (2 * s, 2 * s + 1):
-                    w0 = K0 + D * j + 2 * R * (h - r % 2)
+                    w0 = K0 + 2 * D * h + 2 * R * j - R * quadrant(r, h)
+                    plane = e2[rows(r), w0 + R : w0 + R + D] if quadrant(r, h) % 2 else e1[rows(r), w0 : w0 + D]
                     m0 = S0 + D * h
                     nc.tensor.matmul_mx(
                         out=z_out(r, j),
                         lhsT=c1[rows(r), w0 : w0 + D].bitcast(FP8X4),
-                        lhsT_scale=e1[rows(r), w0 : w0 + D],
+                        lhsT_scale=plane,
                         rhs=c1[rows(r), m0 : m0 + D].bitcast(FP8X4),
                         rhs_scale=e1[rows(r), m0 : m0 + D],
                         start=(h == 0),
@@ -146,7 +184,10 @@ def tile_rows_upd_delta_kernel(tc, kT, S, v, be, kn, out):
 
         def copy_kn(s):
             dst, src = interleave(kn_bf[:, s], kn_raw[:, s])
-            nc.vector.tensor_copy(out=dst, in_=src)
+            if s == 0:
+                nc.vector.tensor_copy(out=dst, in_=src)
+            else:
+                nc.scalar.copy(out=dst, in_=src)
 
         def quantize_kn(s):
             cols = slice(D * s, D * s + D)
@@ -154,15 +195,15 @@ def tile_rows_upd_delta_kernel(tc, kT, S, v, be, kn, out):
 
         def scale_v(s):
             for j in range(PACK):
-                nc.scalar.activation(
-                    out=vbe[:, s, j, :], in_=v_raw[:, s, j, :], func=ACT.Copy, scale=be_t[:, s, j : j + 1]
+                nc.vector.tensor_scalar(
+                    out=vbe[:, s, j, :], in0=v_raw[:, s, j, :], scalar1=be_t[:, s, j, :], scalar2=None, op0=ALU.mult
                 )
 
         def scale_low(s, j0, n):
             nc.vector.tensor_tensor(
                 out=zbe[0:64, s, j0 : j0 + n, :],
                 in0=banks[2 * s][j0 // 2][0:64, 0 : n * D].rearrange("p (j e) -> p j e", j=n),
-                in1=be_t[0:64, s, j0 : j0 + n].unsqueeze(2).to_broadcast([64, n, D]),
+                in1=be_t[0:64, s, j0 : j0 + n, :].to_broadcast([64, n, D]),
                 op=ALU.mult,
             )
 
@@ -173,7 +214,7 @@ def tile_rows_upd_delta_kernel(tc, kT, S, v, be, kn, out):
                     out=zbe[half, r // 2, j, :],
                     in_=banks[r][b][half, D * (j % 2) : D * (j % 2) + D],
                     func=ACT.Copy,
-                    scale=be_t[half, r // 2, j : j + 1],
+                    scale=be_t[half, r // 2, j, :],
                 )
 
         def make_u(s):
@@ -181,9 +222,12 @@ def tile_rows_upd_delta_kernel(tc, kT, S, v, be, kn, out):
             dst, b = interleave(u_bf[:, s], zbe[:, s])
             nc.vector.tensor_tensor(out=dst, in0=a, in1=b, op=ALU.subtract)
 
-        def write_back(s):
+        def quantize_u(s):
             cols = slice(D * s, D * s + D)
             quantize(u_c[:, cols], u_e[:, cols], u_bf[:, s].rearrange("p w j -> p (w j)"))
+
+        def write_back(s):
+            cols = slice(D * s, D * s + D)
             for c in range(TILES):
                 nc.tensor.matmul_mx(
                     out=w_out(c, s),
@@ -195,28 +239,26 @@ def tile_rows_upd_delta_kernel(tc, kT, S, v, be, kn, out):
                     stop=True,
                 )
 
-        def finish(s, k):
-            g0 = 4 * s + 2 * k
-            for g in range(g0, g0 + 2):
-                nc.vector.tensor_tensor(
-                    out=res[:, g, :], in0=w_out(g % 4, s), in1=s_rows[:, g, :], op=ALU.add
-                )
-            nc.sync.dma_start(out=out[g0 : g0 + 2].rearrange("g f e -> f g e"), in_=res[:, g0 : g0 + 2, :])
+        def finish(r):
+            for c in (2 * (r % 2), 2 * (r % 2) + 1):
+                n = 2 * r + (c - 2 if r % 2 else 1 - c)
+                nc.vector.tensor_tensor(out=res[:, n, :], in0=w_out(c, r // 2), in1=s_rows[:, n, :], op=ALU.add)
+            nc.sync.dma_start(out=pair(out, r), in_=res[:, 2 * r : 2 * r + 2, :])
 
-        scale_v(0)
-        scale_v(1)
-        for r, b in ((1, 0), (1, 1), (3, 0), (2, 0), (3, 1)):
+        for r, b in ((1, 0), (1, 1), (3, 0), (2, 0), (3, 1), (2, 1)):
             scale_act(r, b)
-        copy_kn(0)
-        quantize_kn(0)
         copy_kn(1)
+        scale_v(0)
         scale_low(0, 0, 4)
+        scale_v(1)
         make_u(0)
-        scale_low(1, 2, 2)
+        copy_kn(0)
+        quantize_u(0)
+        quantize_kn(0)
         write_back(0)
         make_u(1)
         quantize_kn(1)
+        quantize_u(1)
         write_back(1)
-        for s in range(SETS):
-            for k in range(2):
-                finish(s, k)
+        for r in range(TILES):
+            finish(r)

@@ -56,16 +56,16 @@ def tile_rows_upd_delta_kernel(tc, kT, S, v, be, kn, out):
         res = sb.tile([P, G, D], F32, name="res")
         zeros = sb.tile([P, PAD * PACK], BF16, name="zeros", align_bytes=64)
         warm = ps.tile([P, 512], F32, name="warm")
-        bank0 = ps.tile([P, 512], F32, name="bank0")
-        banks = [[ps.tile([P, 512], F32, name="bank%d%d" % (r, b)) for b in range(2)] if r else [bank0, bank0]
+        lone = ps.tile([P, 512], F32, name="lone")
+        banks = [[ps.tile([P, 512], F32, name="bank%d%d" % (r, b)) for b in range(2)] if r != 2 else [lone, lone]
                  for r in range(TILES)]
 
         def z_out(r, j):
-            c0 = D * j if r == 0 else D * (j % 2)
+            c0 = D * j if r == 2 else D * (j % 2)
             return banks[r][j // 2][:, c0 : c0 + D]
 
         def w_out(c, s):
-            c0 = D * s if c == 0 else 2 * D
+            c0 = D * s if c == 2 else 2 * D
             return banks[c][s][:, c0 : c0 + D]
 
         def pair(t, r):
@@ -80,24 +80,25 @@ def tile_rows_upd_delta_kernel(tc, kT, S, v, be, kn, out):
         def by_rows(src):
             return src.rearrange("c (p j) w -> (c p) j w", j=PACK)
 
-        def load_tokens(eng, dst, src, part):
+        def load_tokens(eng, dst, src, part, sets):
             lo, hi, g0 = ((0, R, 4), (R, 3 * R, 0), (3 * R, P, 5))[part]
             heads = src.rearrange("(h s c) (p j) w -> h c p s j w", h=2, s=SETS, j=PACK)
             if part == 1:
                 view = heads[0].rearrange("c p s j w -> (c p) s j w")
             else:
                 view = heads[1, g0 - 4]
-            eng.dma_start(out=dst[lo:hi], in_=view)
+            eng.dma_start(out=dst[lo:hi, sets], in_=view[:, sets])
 
         for src, dst in ((S, s_raw), (kT, kt_raw)):
             for h in range(2):
                 nc.sync.dma_start(out=dst[:, h], in_=by_rows(src[4 * h : 4 * h + 4]))
         for part in range(3):
-            load_tokens(nc.scalar, be_t, be, part)
-        for src, dst in ((v, v_raw), (kn, kn_raw)):
-            for part in (0, 2, 1):
-                load_tokens(nc.sync, dst, src, part)
-        for r in range(TILES):
+            load_tokens(nc.scalar, be_t, be, part, slice(0, SETS))
+        for s in range(SETS):
+            for src, dst in ((v, v_raw), (kn, kn_raw)):
+                for part in (0, 2, 1):
+                    load_tokens(nc.sync, dst, src, part, slice(s, s + 1))
+        for r in (1, 0, 2, 3):
             nc.sync.dma_start(out=s_rows[:, 2 * r : 2 * r + 2, :], in_=pair(S, r))
 
         def quantize(codes, scales, values):
@@ -212,7 +213,7 @@ def tile_rows_upd_delta_kernel(tc, kT, S, v, be, kn, out):
             for j in range(2 * b, 2 * b + 2):
                 nc.scalar.activation(
                     out=zbe[half, r // 2, j, :],
-                    in_=banks[r][b][half, D * (j % 2) : D * (j % 2) + D],
+                    in_=z_out(r, j)[half],
                     func=ACT.Copy,
                     scale=be_t[half, r // 2, j, :],
                 )
@@ -243,22 +244,27 @@ def tile_rows_upd_delta_kernel(tc, kT, S, v, be, kn, out):
             for c in (2 * (r % 2), 2 * (r % 2) + 1):
                 n = 2 * r + (c - 2 if r % 2 else 1 - c)
                 nc.vector.tensor_tensor(out=res[:, n, :], in0=w_out(c, r // 2), in1=s_rows[:, n, :], op=ALU.add)
-            nc.sync.dma_start(out=pair(out, r), in_=res[:, 2 * r : 2 * r + 2, :])
+                if r == 3:
+                    nc.sync.dma_start(out=out[r + 4 * (n - 2 * r)], in_=res[:, n, :])
+            if r != 3:
+                nc.sync.dma_start(out=pair(out, r), in_=res[:, 2 * r : 2 * r + 2, :])
 
-        for r, b in ((1, 0), (1, 1), (3, 0), (2, 0), (3, 1), (2, 1)):
+        for r, b in ((1, 0), (1, 1), (3, 0), (3, 1), (2, 0), (2, 1)):
             scale_act(r, b)
         copy_kn(1)
         scale_v(0)
-        scale_low(0, 0, 4)
-        scale_v(1)
-        make_u(0)
+        scale_low(0, 0, 2)
+        scale_low(0, 2, 2)
         copy_kn(0)
-        quantize_u(0)
+        make_u(0)
+        scale_v(1)
         quantize_kn(0)
+        quantize_u(0)
         write_back(0)
         make_u(1)
         quantize_kn(1)
         quantize_u(1)
+        finish(1)
         write_back(1)
-        for r in range(TILES):
+        for r in (0, 2, 3):
             finish(r)

from contextlib import ExitStack

import concourse.mybir as mybir

G, D = 8, 128
FLOPS = 2 * 2 * G * D * D * D

F32 = mybir.dt.float32
BF16 = mybir.dt.bfloat16
U32 = mybir.dt.uint32
I32 = mybir.dt.int32
U8 = mybir.dt.uint8
FP8X4 = mybir.dt.float8_e4m3fn_x4
ALU = mybir.AluOpType
ACT = mybir.ActivationFunctionType

P = 128
R = 32
PACK = 4
TILES = 4
SETS = 2
PAD = 128
WARM_EARLY = 28
WARM_LATE = 8
K0 = PAD
S0 = PAD + PACK * D
S_SPLIT = 32


def tile_rows_upd_delta_kernel(tc, kT, S, v, be, kn, out):
    nc = tc.nc
    with ExitStack() as ctx:
        sb = ctx.enter_context(tc.tile_pool(name="sb", bufs=1))
        ps = ctx.enter_context(tc.psum_pool(name="ps", bufs=1))
        ctx.enter_context(tc.manual_schedule())

        kt_raw = sb.tile([P, 2, PACK, D], F32, name="kt_raw")
        s_raw = sb.tile([P, 2, PACK, D], F32, name="s_raw")
        kn_raw = sb.tile([P, SETS, PACK, D], F32, name="kn_raw")
        v_raw = sb.tile([P, SETS, PACK, D], F32, name="v_raw")
        s_rows = sb.tile([P, G, D], F32, name="s_rows")
        be_t = sb.tile([P, SETS, PACK, 1], F32, name="be_t")
        kt_bf = sb.tile([P, 2, PACK, 2, R, PACK], BF16, name="kt_bf", align_bytes=64)
        s_bf = sb.tile([P, 2, D, PACK], BF16, name="s_bf", align_bytes=64)
        kn_bf = sb.tile([P, SETS, D, PACK], BF16, name="kn_bf", align_bytes=64)
        u_bf = sb.tile([P, SETS, D, PACK], BF16, name="u_bf", align_bytes=64)
        c1 = sb.tile([P, S0 + 2 * D], U32, name="c1", align_bytes=64)
        e1 = sb.tile([P, S0 + 2 * D], U8, name="e1", align_bytes=64)
        e2 = sb.tile([P, S0 + R], U8, name="e2", align_bytes=64)
        kn_c = sb.tile([P, SETS * D], U32, name="kn_c", align_bytes=64)
        kn_e = sb.tile([P, SETS * D], U8, name="kn_e", align_bytes=64)
        u_c = sb.tile([P, SETS * D], U32, name="u_c", align_bytes=64)
        u_e = sb.tile([P, SETS * D], U8, name="u_e", align_bytes=64)
        vbe = sb.tile([P, SETS, PACK, D], F32, name="vbe")
        zbe = sb.tile([P, SETS, PACK, D], F32, name="zbe")
        res = sb.tile([P, G, D], F32, name="res")
        zeros = sb.tile([P, PAD * PACK], BF16, name="zeros", align_bytes=64)
        warm = ps.tile([P, 512], F32, name="warm")
        lone = ps.tile([P, 512], F32, name="lone")
        banks = [[ps.tile([P, 512], F32, name="bank%d%d" % (r, b)) for b in range(2)] if r != 2 else [lone, lone]
                 for r in range(TILES)]

        def z_out(r, j):
            c0 = D * j if r == 2 else D * (j % 2)
            return banks[r][j // 2][:, c0 : c0 + D]

        def w_out(c, s):
            c0 = D * s if c == 2 else 2 * D
            return banks[c][s][:, c0 : c0 + D]

        def pair(t, r):
            return t[r : r + 5 : 4].rearrange("g f e -> f g e")

        def quadrant(r, h):
            return 2 + h if r % 2 else 1 - h

        def rows(r):
            return slice(R * r, R * r + R)

        def by_rows(src):
            return src.rearrange("c (p j) w -> (c p) j w", j=PACK)

        def load_tokens(eng, dst, src, part, sets):
            lo, hi, g0 = ((0, R, 4), (R, 3 * R, 0), (3 * R, P, 5))[part]
            heads = src.rearrange("(h s c) (p j) w -> h c p s j w", h=2, s=SETS, j=PACK)
            if part == 1:
                view = heads[0].rearrange("c p s j w -> (c p) s j w")
            else:
                view = heads[1, g0 - 4]
            eng.dma_start(out=dst[lo:hi, sets], in_=view[:, sets])

        for src, dst in ((S, s_raw), (kT, kt_raw)):
            for h in range(2):
                nc.sync.dma_start(out=dst[:, h], in_=by_rows(src[4 * h : 4 * h + 4]))
        for part in range(3):
            load_tokens(nc.scalar, be_t, be, part, slice(0, SETS))
        for s in range(SETS):
            for src, dst in ((v, v_raw), (kn, kn_raw)):
                for part in (0, 2, 1):
                    load_tokens(nc.sync, dst, src, part, slice(s, s + 1))
        for r in (1, 0, 2, 3):
            nc.sync.dma_start(out=s_rows[:, 2 * r : 2 * r + 2, :], in_=pair(S, r))

        def quantize(codes, scales, values):
            nc.vector.quantize_mx(out=codes.bitcast(FP8X4), scales=scales, in_=values)

        def warm_up(w0, passes):
            for i in range(passes):
                nc.tensor.matmul_mx(
                    out=warm[:, D * (i % 4) : D * (i % 4) + D],
                    lhsT=c1[:, w0 : w0 + D].bitcast(FP8X4),
                    lhsT_scale=e1[:, w0 : w0 + D],
                    rhs=c1[:, w0 : w0 + D].bitcast(FP8X4),
                    rhs_scale=e1[:, w0 : w0 + D],
                    start=True,
                    stop=True,
                )

        nc.vector.memset(zeros[:].bitcast(U32), 0)
        blocks = kt_bf[:].rearrange("p h a z t j -> p (h a) z (t j)")
        nc.vector.memset(blocks[:, 0:6, 1, :].bitcast(U32), 0)
        quantize(c1[:, 0:PAD], e1[:, 0:PAD], zeros[:])
        nc.vector.memset(e1[:, K0:S0].bitcast(I32), 0)
        nc.vector.memset(e2[:].bitcast(I32), 0)
        nc.scalar.activation(
            out=blocks[:, 6:8, 1, :], in_=zeros[:, 0 : 2 * R * PACK].rearrange("p (a w) -> p a w", a=2), func=ACT.Copy
        )
        warm_up(0, WARM_EARLY)

        def deal_kt(h, a):
            dst = kt_bf[:, h, 2 * a : 2 * a + 2, 0].rearrange("p b t d -> p t d b")
            src = kt_raw[:, h].rearrange("p d (t a b) -> p a t d b", a=2, b=2)[:, a]
            return dst, src

        def interleave(dst, src):
            return (dst.rearrange("p (c i) j -> p c j i", i=2), src.rearrange("p j (c i) -> p c j i", i=2))

        for h in range(2):
            d0, s0 = interleave(s_bf[:, h], s_raw[:, h])
            nc.vector.tensor_copy(out=d0, in_=s0)
        quantize(c1[:, S0:], e1[:, S0:], s_bf[:].rearrange("p h w j -> p (h w j)"))
        warm_up(S0, WARM_LATE)

        d0, s0 = deal_kt(0, 0)
        nc.vector.tensor_copy(out=d0, in_=s0)
        d0, s0 = deal_kt(0, 1)
        nc.scalar.copy(out=d0, in_=s0)

        def quantize_kt(h, a0, n):
            words = slice(K0 + 2 * D * h + D * a0, K0 + 2 * D * h + D * (a0 + n))
            values = kt_bf[:, h, 2 * a0 : 2 * (a0 + n)].rearrange("p a z t j -> p (a z t j)")
            quantize(c1[:, words], e1[:, words], values)

        def shift_scales(h, a0, n):
            w0 = K0 + 2 * D * h + D * a0
            nc.vector.tensor_copy(
                out=e2[:, w0 + R : w0 + R + D * n].bitcast(I32), in_=e1[:, w0 : w0 + D * n].bitcast(I32)
            )

        quantize_kt(0, 0, 2)
        shift_scales(0, 0, 2)
        for a in range(2):
            d0, s0 = deal_kt(1, a)
            nc.vector.tensor_copy(out=d0, in_=s0)
        for a in range(2):
            quantize_kt(1, a, 1)
        for a in range(2):
            shift_scales(1, a, 1)

        for s, j in [(s, j) for s in range(SETS) for j in range(PACK)]:
            for h in range(2):
                for r in (2 * s, 2 * s + 1):
                    w0 = K0 + 2 * D * h + 2 * R * j - R * quadrant(r, h)
                    plane = e2[rows(r), w0 + R : w0 + R + D] if quadrant(r, h) % 2 else e1[rows(r), w0 : w0 + D]
                    m0 = S0 + D * h
                    nc.tensor.matmul_mx(
                        out=z_out(r, j),
                        lhsT=c1[rows(r), w0 : w0 + D].bitcast(FP8X4),
                        lhsT_scale=plane,
                        rhs=c1[rows(r), m0 : m0 + D].bitcast(FP8X4),
                        rhs_scale=e1[rows(r), m0 : m0 + D],
                        start=(h == 0),
                        stop=(h == 1),
                    )

        def copy_kn(s):
            dst, src = interleave(kn_bf[:, s], kn_raw[:, s])
            if s == 0:
                nc.vector.tensor_copy(out=dst, in_=src)
            else:
                nc.scalar.copy(out=dst, in_=src)

        def quantize_kn(s):
            cols = slice(D * s, D * s + D)
            quantize(kn_c[:, cols], kn_e[:, cols], kn_bf[:, s].rearrange("p w j -> p (w j)"))

        def scale_v(s):
            for j in range(PACK):
                nc.vector.tensor_scalar(
                    out=vbe[:, s, j, :], in0=v_raw[:, s, j, :], scalar1=be_t[:, s, j, :], scalar2=None, op0=ALU.mult
                )

        def scale_low(s, j0, n):
            nc.vector.tensor_tensor(
                out=zbe[0:64, s, j0 : j0 + n, :],
                in0=banks[2 * s][j0 // 2][0:64, 0 : n * D].rearrange("p (j e) -> p j e", j=n),
                in1=be_t[0:64, s, j0 : j0 + n, :].to_broadcast([64, n, D]),
                op=ALU.mult,
            )

        def scale_act(r, b):
            half = slice(64 * (r % 2), 64 * (r % 2) + 64)
            for j in range(2 * b, 2 * b + 2):
                nc.scalar.activation(
                    out=zbe[half, r // 2, j, :],
                    in_=z_out(r, j)[half],
                    func=ACT.Copy,
                    scale=be_t[half, r // 2, j, :],
                )

        def make_u(s):
            dst, a = interleave(u_bf[:, s], vbe[:, s])
            dst, b = interleave(u_bf[:, s], zbe[:, s])
            nc.vector.tensor_tensor(out=dst, in0=a, in1=b, op=ALU.subtract)

        def quantize_u(s):
            cols = slice(D * s, D * s + D)
            quantize(u_c[:, cols], u_e[:, cols], u_bf[:, s].rearrange("p w j -> p (w j)"))

        def write_back(s):
            cols = slice(D * s, D * s + D)
            for c in range(TILES):
                nc.tensor.matmul_mx(
                    out=w_out(c, s),
                    lhsT=kn_c[rows(c), cols].bitcast(FP8X4),
                    lhsT_scale=kn_e[rows(c), cols],
                    rhs=u_c[rows(c), cols].bitcast(FP8X4),
                    rhs_scale=u_e[rows(c), cols],
                    start=True,
                    stop=True,
                )

        def finish(r):
            for c in (2 * (r % 2), 2 * (r % 2) + 1):
                n = 2 * r + (c - 2 if r % 2 else 1 - c)
                nc.vector.tensor_tensor(out=res[:, n, :], in0=w_out(c, r // 2), in1=s_rows[:, n, :], op=ALU.add)
                if r == 3:
                    nc.sync.dma_start(out=out[r + 4 * (n - 2 * r)], in_=res[:, n, :])
            if r != 3:
                nc.sync.dma_start(out=pair(out, r), in_=res[:, 2 * r : 2 * r + 2, :])

        for r, b in ((1, 0), (1, 1), (3, 0), (3, 1), (2, 0), (2, 1)):
            scale_act(r, b)
        copy_kn(1)
        scale_v(0)
        scale_low(0, 0, 2)
        scale_low(0, 2, 2)
        copy_kn(0)
        make_u(0)
        scale_v(1)
        quantize_kn(0)
        quantize_u(0)
        write_back(0)
        make_u(1)
        quantize_kn(1)
        quantize_u(1)
        finish(1)
        write_back(1)
        for r in (0, 2, 3):
            finish(r)
